import numpy as np
import ml_dtypes


def mxq(x, axis, fmt="e4m3"):
    dtype, down = {"e4m3": (ml_dtypes.float8_e4m3fn, 7), "e5m2": (ml_dtypes.float8_e5m2, 14)}[fmt]
    v = np.moveaxis(np.asarray(x, np.float32).astype(ml_dtypes.bfloat16).astype(np.float64), axis, -1)
    blocks = v.reshape(v.shape[:-1] + (-1, 32))
    amax = np.abs(blocks).max(-1, keepdims=True)
    byte = np.maximum(np.where(amax > 0, np.frexp(amax)[1] - 1 + 127, 0) - down, 1)
    scale = np.exp2(byte - 127.0)
    codes = (blocks / scale).astype(np.float32).astype(dtype).astype(np.float64)
    return np.moveaxis((codes * scale).reshape(v.shape), -1, axis)


WIDE = False


def mx_kscale(k):
    if not WIDE:
        return np.ones(k)
    levels = np.array([10, -10, 5, -5, 0])
    if k % 512:
        return np.exp2(np.random.permutation(np.resize(levels, k // 32))).repeat(32)
    a = np.empty((k // 512, 16))
    for p in range(k // 512):
        a[p, :8] = np.random.permutation(np.resize(levels, 8))
        for g in range(8):
            far = levels[np.abs(levels - a[p, g]) >= 10]
            a[p, g + 8] = far[np.random.randint(len(far))]
    return np.exp2(a.ravel()).repeat(32)


def f64(x):
    return np.asarray(x).astype(np.float64)


def striped(idx):
    return np.tile(idx.reshape(-1, 16).T, (8, 1)).astype(np.uint16)


def unstriped(offs):
    return offs[:16].T.reshape(-1).astype(np.int64)


def pack_weight(w):
    k, n = w.shape
    w = f64(np.asarray(w, np.float32).astype(ml_dtypes.bfloat16)).reshape(k // 32, 32, n)
    amax = np.abs(w).max(1)
    byte = np.clip(np.where(amax > 0, np.frexp(amax)[1] - 1 + 127 - 7, 1), 1, 254)
    scaled = (w * np.exp2(127.0 - byte)[:, None, :]).reshape(k, n).astype(np.float32)
    words = np.ascontiguousarray(scaled.reshape(k // 512, 128, 4, n).transpose(0, 1, 3, 2)).astype(ml_dtypes.float8_e4m3fn).view(np.uint8)
    return words, np.ascontiguousarray(byte.astype(np.uint8).reshape(k // 512, 16, n))


def unpack_weight(words, scales):
    g, p, n, _ = words.shape
    vals = np.ascontiguousarray(words).view(ml_dtypes.float8_e4m3fn).astype(np.float64) * np.repeat(np.exp2(scales.astype(np.float64) - 127.0), 8, axis=1)[..., None]
    return vals.transpose(0, 1, 3, 2).reshape(g * 512, n)


def silu(v):
    return v / (1.0 + np.exp(-np.maximum(v, -700.0)))


K, T, E, C, N = 1024, 640, 5, 256, 384
M = 1024


def by_expert(wq, xq):
    return np.concatenate([wq[e].T @ xq[:, e * C:(e + 1) * C] for e in range(E)], axis=1)


def setup_inputs():
    n = np.random.standard_normal
    s = mx_kscale(K)[:, None]
    first = np.random.permutation(np.repeat(np.arange(E), T // E))
    second = (first + 1 + np.random.permutation(np.repeat(np.arange(E - 1), -(-T // (E - 1)))[:T])) % E
    while np.bincount(second, minlength=E).max() != T // E:
        load = np.bincount(second, minlength=E); hi, lo = int(load.argmax()), int(load.argmin())
        t = np.flatnonzero((second == hi) & (first != lo))[0]; second[t] = lo
    slot_token = np.empty(E * C, np.int64); pos = np.empty((2, T), np.int64); fill = np.zeros(E, np.int64)
    place = np.stack([np.random.permutation(C) for _ in range(E)])
    for r, deal in enumerate((first, second)):
        for t in np.random.permutation(T):
            e = deal[t]; j = e * C + place[e, fill[e]]; fill[e] += 1; slot_token[j] = t; pos[r, t] = j
    g = np.random.uniform(0.2, 0.8, T)
    packed = [pack_weight(m) for m in n((E, K, N)) / np.sqrt(K) / s[None]]
    r = mx_kscale(M)[:, None]
    return {
        "uT": (n((M, T)) * r).astype(np.float32),
        "wu": (n((M, K)) / np.sqrt(M) / r * s.T).astype(np.float32),
        "w_words": np.stack([m[0] for m in packed]),
        "w_scales": np.stack([m[1] for m in packed]),
        "b": (0.3 * n((N, E))).astype(np.float32),
        "gate": np.stack([np.tile(g, (N, 1)), np.tile(1.0 - g, (N, 1))]).astype(np.float32),
        "offs": striped(slot_token),
        "pos1": striped(pos[0]),
        "pos2": striped(pos[1]),
    }


def reference(uT, wu, w_words, w_scales, b, gate, offs, pos1, pos2):
    idx = unstriped(offs)
    w = np.stack([unpack_weight(w_words[e], w_scales[e]) for e in range(E)])
    x = mxq(f64(wu), 0, "e4m3").T @ mxq(f64(uT), 0, "e4m3")
    xq = mxq(x[:, idx], 0, "e4m3")
    y = by_expert(w, xq)
    y = silu(y + np.repeat(f64(b), C, axis=1))
    return f64(gate[0]) * y[:, unstriped(pos1)] + f64(gate[1]) * y[:, unstriped(pos2)]

@@ -1,0 +1,238 @@
+from contextlib import ExitStack
+
+import concourse.mybir as mybir
+
+M, K, T, E, C, N = 1024, 1024, 640, 5, 256, 384
+S = E * C
+
+F32 = mybir.dt.float32
+BF16 = mybir.dt.bfloat16
+I32 = mybir.dt.int32
+U32 = mybir.dt.uint32
+U16 = mybir.dt.uint16
+U8 = mybir.dt.uint8
+FP8X4 = mybir.dt.float8_e4m3fn_x4
+MULT = mybir.AluOpType.mult
+ADD = mybir.AluOpType.add
+SILU = mybir.ActivationFunctionType.Silu
+
+P = 128
+PASS = 512
+WINDOW = 704
+TOKEN_CHUNKS = ((0, 256), (256, 256), (512, 128))
+SLOT_CHUNKS = (
+    ((0, 512), (512, 256), (768, 256), (1024, 256)),
+    ((0, 512), (512, 512), (1024, 256)),
+)
+ROW_BLOCKS = N // P
+
+FLOPS = 2 * M * K * T + 2 * K * N * S
+BYTES = 4 * (M * T + M * K + N * E + 2 * T + N * T) + E * K * N + E * K * N // 32 + 2 * P * (S + 2 * T) // 16
+
+
+def tile_moe_prv_lin_silu_kernel(
+    tc, uT, wu, w_words, w_scales, b, gate, offs, pos1, pos2, out
+):
+    nc = tc.nc
+    with ExitStack() as ctx:
+        keep = ctx.enter_context(tc.tile_pool(name="keep", bufs=1))
+        psum = ctx.enter_context(tc.psum_pool(name="psum", bufs=1))
+
+        def sb(name, shape, dtype, tag=None):
+            return keep.tile(shape, dtype, name=name, tag=tag or name, align_bytes=64)
+
+        def quantize(name, grouped, width):
+            codes = sb(name + "_codes", [P, width], U32)
+            scales = sb(name + "_scales", [P, width], U8)
+            nc.vector.quantize_mx(out=codes[:].bitcast(FP8X4), scales=scales[:], in_=grouped)
+            return codes, scales
+
+        wu_raw = {}
+        u_raw = {}
+
+        def load_wu(a, f):
+            raw = sb(f"wu_raw{a}{f}", [P, 4, PASS], F32)
+            rows = wu[f * PASS : (f + 1) * PASS, a * PASS : (a + 1) * PASS]
+            nc.sync.dma_start(out=raw[:], in_=rows.rearrange("(p j) c -> p j c", j=4))
+            wu_raw[a, f] = raw
+
+        load_wu(0, 0)
+        load_wu(0, 1)
+        for c, (t0, n) in enumerate(TOKEN_CHUNKS):
+            for f in range(2):
+                raw = sb(f"u_raw{f}{c}", [P, 4, n], F32)
+                rows = uT[f * PASS : (f + 1) * PASS, t0 : t0 + n]
+                nc.sync.dma_start(out=raw[:], in_=rows.rearrange("(p j) t -> p j t", j=4))
+                u_raw[f, c] = raw
+        offs_sb = sb("offs_sb", [P, S // 16], U16)
+        nc.sync.dma_start(offs_sb[:], offs)
+        load_wu(1, 0)
+        load_wu(1, 1)
+
+        w_sb = []
+        for e in range(E):
+            words = sb(f"w_words{e}", [P, 2, N], U32)
+            nc.sync.dma_start(
+                out=words[:].bitcast(I32),
+                in_=w_words[e].rearrange("a p n r -> p a (n r)").bitcast(I32),
+            )
+            w_sb.append(words)
+        w_sc = sb("w_sc", [P, 2 * E, N], U8)
+        nc.gpsimd.memset(w_sc[:].bitcast(I32), 0)
+        sc_rows = w_scales.rearrange("e a (g r) n -> r g (e a) n", r=4)
+        for r in range(4):
+            nc.sync.dma_start(out=w_sc[r:P:32].bitcast(I32), in_=sc_rows[r].bitcast(I32))
+        b_sb = sb("b_sb", [P, ROW_BLOCKS, E], F32)
+        nc.sync.dma_start(out=b_sb[:], in_=b.rearrange("(r p) e -> p r e", p=P))
+        pos_sb = []
+        for i, pos in enumerate((pos1, pos2)):
+            lst = sb(f"pos_sb{i}", [P, T // 16], U16)
+            nc.sync.dma_start(lst[:], pos)
+            pos_sb.append(lst)
+        gate_sb = sb("gate_sb", [P, 2, T], F32)
+        nc.sync.dma_start(out=gate_sb[:], in_=gate[:, 0:P, :].rearrange("i p t -> p i t"))
+
+        win = {}
+        for a in range(2):
+            for u in range(2):
+                tile = sb(f"win{a}{u}", [P, 2 * WINDOW], BF16)
+                nc.gpsimd.memset(tile[:, 2 * T :], 0.0)
+                win[a, u] = tile
+
+        wq = {}
+        uq = {}
+
+        def cast_wu(a, f, u, copy):
+            grouped = sb(f"wu_g{a}{f}{u}", [P, 2, P, 4], BF16)
+            src = wu_raw[a, f][:].rearrange("p j (m t) -> p m j t", t=4)[:, :, :, 2 * u : 2 * u + 2]
+            copy(out=grouped[:].rearrange("p t m j -> p m j t"), in_=src)
+            return grouped[:].rearrange("p t m j -> p (t m j)")
+
+        def cast_u(f, c, copy):
+            n = TOKEN_CHUNKS[c][1]
+            grouped = sb(f"u_g{f}{c}", [P, n, 4], BF16)
+            copy(
+                out=grouped[:].rearrange("p (c i) j -> p c j i", i=4),
+                in_=u_raw[f, c][:].rearrange("p j (c i) -> p c j i", i=4),
+            )
+            return grouped[:].rearrange("p t j -> p (t j)")
+
+        def project(a, u, c):
+            t0, n = TOKEN_CHUNKS[c]
+            bank = psum.tile([P, 2, n], F32, name="proj", tag="proj", bufs=4)
+            for tt in range(2):
+                cols = slice(tt * P, (tt + 1) * P)
+                for f in range(2):
+                    nc.tensor.matmul_mx(
+                        out=bank[:, tt, :],
+                        lhsT=wq[a, f, u][0][:, cols].bitcast(FP8X4),
+                        lhsT_scale=wq[a, f, u][1][:, cols],
+                        rhs=uq[f, c][0][:].bitcast(FP8X4),
+                        rhs_scale=uq[f, c][1][:],
+                        start=(f == 0),
+                        stop=(f == 1),
+                    )
+            nc.scalar.copy(
+                out=win[a, u][:, 2 * t0 : 2 * (t0 + n)].rearrange("p (n t) -> p n t", t=2),
+                in_=bank[:].rearrange("p t n -> p n t"),
+            )
+
+        both = (nc.vector.tensor_copy, nc.scalar.copy)
+        for f in range(2):
+            g = [cast_wu(0, f, u, both[u]) for u in range(2)]
+            for u in range(2):
+                wq[0, f, u] = quantize(f"wq0{f}{u}", g[u], 2 * P)
+        for c, (t0, n) in enumerate(TOKEN_CHUNKS):
+            g = [cast_u(f, c, nc.vector.tensor_copy) for f in range(2)]
+            for f in range(2):
+                uq[f, c] = quantize(f"uq{f}{c}", g[f], n)
+            for u in range(2):
+                project(0, u, c)
+
+        pairs = {}
+        xq = {}
+
+        def gather(a, u, c, tag=None):
+            s0, n = SLOT_CHUNKS[a][c]
+            if u == 0:
+                pairs[a, c] = sb(f"pairs{a}{c}", [P, 2, n], U32, tag)
+            nc.vector.tensor_copy(
+                out=pairs[a, c][:, u, :],
+                in_=win[a, u][:].bitcast(U32).indirect(offs_sb[:, s0 // 16 : (s0 + n) // 16]),
+            )
+
+        def weave(a, c, tag=None):
+            n = SLOT_CHUNKS[a][c][1]
+            quads = sb(f"quads{a}{c}", [P, 4 * n], BF16, tag)
+            nc.scalar.copy(
+                out=quads[:].bitcast(U32).rearrange("p (n u) -> p n u", u=2),
+                in_=pairs[a, c][:].rearrange("p u n -> p n u"),
+            )
+            return quads
+
+        def quantize_slots(a, c, quads):
+            s0, n = SLOT_CHUNKS[a][c]
+            codes, scales = quantize(f"xq{a}{c}", quads[:], n)
+            for e in range(s0 // C, (s0 + n) // C):
+                slots = slice(e * C - s0, (e + 1) * C - s0)
+                xq[a, e] = (codes[:, slots], scales[:, slots])
+
+        g1 = {}
+        for f in range(2):
+            for u in range(2):
+                g1[f, u] = cast_wu(1, f, u, nc.scalar.copy)
+        for u in range(2):
+            gather(0, u, 0)
+        for c, done in ((1, ((0, 0), (0, 1))), (2, ((1, 0),)), (3, ((1, 1),))):
+            for f, u in done:
+                wq[1, f, u] = quantize(f"wq1{f}{u}", g1[f, u], 2 * P)
+            f, u = done[-1]
+            gather(0, 0, c, f"wu_g1{f}{u}")
+            gather(0, 1, c)
+        for u in range(2):
+            for c in range(3):
+                project(1, u, c)
+        for u in range(2):
+            for c in range(3):
+                gather(1, u, c)
+        late = ("uq02_codes", "uq12_codes", "wq101_codes", "wq111_codes")
+        quads = {}
+        for c in range(4):
+            quads[0, c] = weave(0, c, late[c])
+        for c in range(3):
+            quads[1, c] = weave(1, c)
+        for a in range(2):
+            for c in range(len(SLOT_CHUNKS[a])):
+                quantize_slots(a, c, quads[a, c])
+
+        y = [sb(f"y{r}", [P, S], F32) for r in range(ROW_BLOCKS)]
+        for r in range(ROW_BLOCKS):
+            cols = slice(r * P, (r + 1) * P)
+            for e in range(E):
+                bank = psum.tile([P, C], F32, name="ybank", tag="ybank", bufs=3)
+                for a in range(2):
+                    nc.tensor.matmul_mx(
+                        out=bank[:],
+                        lhsT=w_sb[e][:, a, cols].bitcast(FP8X4),
+                        lhsT_scale=w_sc[:, 2 * e + a, cols],
+                        rhs=xq[a, e][0].bitcast(FP8X4),
+                        rhs_scale=xq[a, e][1],
+                        start=(a == 0),
+                        stop=(a == 1),
+                    )
+                nc.scalar.activation(
+                    out=y[r][:, e * C : (e + 1) * C], in_=bank[:], func=SILU, bias=b_sb[:, r, e : e + 1]
+                )
+
+        for r in range(ROW_BLOCKS):
+            pieces = ((0, T),) if r + 1 < ROW_BLOCKS else ((0, 384), (384, 256))
+            for t0, n in pieces:
+                parts = []
+                for i in range(2):
+                    part = sb(f"part{r}{i}{t0}", [P, n], F32)
+                    picked = y[r][:].indirect(pos_sb[i][:, t0 // 16 : (t0 + n) // 16])
+                    nc.vector.tensor_tensor(part[:], picked, gate_sb[:, i, t0 : t0 + n], MULT)
+                    parts.append(part)
+                total = sb(f"total{r}{t0}", [P, n], F32)
+                nc.vector.tensor_tensor(total[:], parts[0][:], parts[1][:], ADD)
+                nc.sync.dma_start(out=out[r * P : (r + 1) * P, t0 : t0 + n], in_=total[:])

@@ -1,6 +1,7 @@
 from contextlib import ExitStack
 
 import concourse.mybir as mybir
+from concourse.masks import make_identity
 
 M, K, T, E, C, N = 1024, 1024, 640, 5, 256, 384
 S = E * C
@@ -15,16 +16,22 @@ FP8X4 = mybir.dt.float8_e4m3fn_x4
 MULT = mybir.AluOpType.mult
 ADD = mybir.AluOpType.add
 SILU = mybir.ActivationFunctionType.Silu
+COPY = mybir.ActivationFunctionType.Copy
 
 P = 128
 PASS = 512
 WINDOW = 704
 TOKEN_CHUNKS = ((0, 256), (256, 256), (512, 128))
 SLOT_CHUNKS = (
-    ((0, 512), (512, 256), (768, 256), (1024, 256)),
+    ((0, 512), (512, 256), (768, 512)),
     ((0, 512), (512, 512), (1024, 256)),
 )
+U_LOADS = (((0, T),), ((0, 384), (384, 256)))
+U_CASTS = (((0, 0, 256, 0), (1, 128, 256, 1), (1, 0, 128, 0), (2, 0, 128, 1)), ((0, 0, 256, 0), (1, 0, 128, 1), (1, 128, 256, 0), (2, 0, 128, 1)))
+V_EVAC = ((0, 1),)
 ROW_BLOCKS = N // P
+BLOCKS = T // P
+BLOCK_GROUPS = ((0, 3), (3, 2))
 
 FLOPS = 2 * M * K * T + 2 * K * N * S
 BYTES = 4 * (M * T + M * K + N * E + 2 * T + N * T) + E * K * N + E * K * N // 32 + 2 * P * (S + 2 * T) // 16
@@ -47,6 +54,13 @@ def tile_moe_prv_lin_silu_kernel(
             nc.vector.quantize_mx(out=codes[:].bitcast(FP8X4), scales=scales[:], in_=grouped)
             return codes, scales
 
+        taken = []
+
+        def bank_tile(shape, bank=None):
+            bank = len(taken) % 8 if bank is None else bank
+            taken.append(bank)
+            return psum.tile(shape, F32, name=f"bank{bank}", tag=f"bank{bank}")
+
         wu_raw = {}
         u_raw = {}
 
@@ -58,14 +72,23 @@ def tile_moe_prv_lin_silu_kernel(
 
         load_wu(0, 0)
         load_wu(0, 1)
-        for c, (t0, n) in enumerate(TOKEN_CHUNKS):
-            for f in range(2):
-                raw = sb(f"u_raw{f}{c}", [P, 4, n], F32)
+        for f in range(2):
+            for t0, n in U_LOADS[f]:
+                raw = sb(f"u_raw{f}{t0}", [P, 4, n], F32)
                 rows = uT[f * PASS : (f + 1) * PASS, t0 : t0 + n]
                 nc.sync.dma_start(out=raw[:], in_=rows.rearrange("(p j) t -> p j t", j=4))
-                u_raw[f, c] = raw
+                for t in range(t0, t0 + n, P):
+                    u_raw[f, t] = (raw, t0)
         offs_sb = sb("offs_sb", [P, S // 16], U16)
         nc.sync.dma_start(offs_sb[:], offs)
+        gate_rows = sb("gate_rows", [P, P], F32)
+        nc.gpsimd.memset(gate_rows[:], 0.0)
+        for i in range(2):
+            nc.sync.dma_start(
+                out=gate_rows[8 * i : 8 * i + BLOCKS, :], in_=gate[i, 0, :].rearrange("(c p) -> c p", p=P)
+            )
+        ident = sb("ident", [P, P], F32)
+        make_identity(nc, ident[:])
         load_wu(1, 0)
         load_wu(1, 1)
 
@@ -102,24 +125,26 @@ def tile_moe_prv_lin_silu_kernel(
         wq = {}
         uq = {}
 
-        def cast_wu(a, f, u, copy):
-            grouped = sb(f"wu_g{a}{f}{u}", [P, 2, P, 4], BF16)
+        def cast_wu(a, f, u, copy, tag=None):
+            grouped = sb(f"wu_g{a}{f}{u}", [P, 2, P, 4], BF16, tag)
             src = wu_raw[a, f][:].rearrange("p j (m t) -> p m j t", t=4)[:, :, :, 2 * u : 2 * u + 2]
             copy(out=grouped[:].rearrange("p t m j -> p m j t"), in_=src)
             return grouped[:].rearrange("p t m j -> p (t m j)")
 
-        def cast_u(f, c, copy):
-            n = TOKEN_CHUNKS[c][1]
-            grouped = sb(f"u_g{f}{c}", [P, n, 4], BF16)
-            copy(
-                out=grouped[:].rearrange("p (c i) j -> p c j i", i=4),
-                in_=u_raw[f, c][:].rearrange("p j (c i) -> p c j i", i=4),
-            )
-            return grouped[:].rearrange("p t j -> p (t j)")
+        def cast_u(f):
+            grouped = [sb(f"u_g{f}{c}", [P, n, 4], BF16) for c, (t0, n) in enumerate(TOKEN_CHUNKS)]
+            for c, lo, hi, engine in U_CASTS[f]:
+                raw, first = u_raw[f, TOKEN_CHUNKS[c][0] + lo]
+                t0 = TOKEN_CHUNKS[c][0] - first
+                (nc.vector.tensor_copy, nc.scalar.copy)[engine](
+                    out=grouped[c][:, lo:hi, :].rearrange("p (c i) j -> p c j i", i=4),
+                    in_=raw[:, :, t0 + lo : t0 + hi].rearrange("p j (c i) -> p c j i", i=4),
+                )
+            return [g[:].rearrange("p t j -> p (t j)") for g in grouped]
 
-        def project(a, u, c):
+        def project(a, u, c, copy=nc.scalar.copy):
             t0, n = TOKEN_CHUNKS[c]
-            bank = psum.tile([P, 2, n], F32, name="proj", tag="proj", bufs=4)
+            bank = bank_tile([P, 2, n])
             for tt in range(2):
                 cols = slice(tt * P, (tt + 1) * P)
                 for f in range(2):
@@ -132,7 +157,7 @@ def tile_moe_prv_lin_silu_kernel(
                         start=(f == 0),
                         stop=(f == 1),
                     )
-            nc.scalar.copy(
+            copy(
                 out=win[a, u][:, 2 * t0 : 2 * (t0 + n)].rearrange("p (n t) -> p n t", t=2),
                 in_=bank[:].rearrange("p t n -> p n t"),
             )
@@ -142,12 +167,18 @@ def tile_moe_prv_lin_silu_kernel(
             g = [cast_wu(0, f, u, both[u]) for u in range(2)]
             for u in range(2):
                 wq[0, f, u] = quantize(f"wq0{f}{u}", g[u], 2 * P)
-        for c, (t0, n) in enumerate(TOKEN_CHUNKS):
-            g = [cast_u(f, c, nc.vector.tensor_copy) for f in range(2)]
-            for f in range(2):
-                uq[f, c] = quantize(f"uq{f}{c}", g[f], n)
-            for u in range(2):
-                project(0, u, c)
+        for f in range(2):
+            g = cast_u(f)
+            for c in range(3):
+                uq[f, c] = quantize(f"uq{f}{c}", g[c], TOKEN_CHUNKS[c][1])
+        for u in range(2):
+            for c in range(3):
+                project(0, u, c, nc.vector.tensor_copy if (u, c) in V_EVAC else nc.scalar.copy)
+
+        gate_bank = bank_tile([P, P], 5)
+        nc.tensor.transpose(gate_bank[:], gate_rows[:], ident[:])
+        gate_cols = sb("gate_cols", [P, 16], F32)
+        nc.scalar.copy(out=gate_cols[:], in_=gate_bank[:, 0:16])
 
         pairs = {}
         xq = {}
@@ -161,12 +192,12 @@ def tile_moe_prv_lin_silu_kernel(
                 in_=win[a, u][:].bitcast(U32).indirect(offs_sb[:, s0 // 16 : (s0 + n) // 16]),
             )
 
-        def weave(a, c, tag=None):
+        def weave(a, c, tag=None, copy=nc.scalar.copy, word=U32):
             n = SLOT_CHUNKS[a][c][1]
             quads = sb(f"quads{a}{c}", [P, 4 * n], BF16, tag)
-            nc.scalar.copy(
-                out=quads[:].bitcast(U32).rearrange("p (n u) -> p n u", u=2),
-                in_=pairs[a, c][:].rearrange("p u n -> p n u"),
+            copy(
+                out=quads[:].bitcast(word).rearrange("p (n u) -> p n u", u=2),
+                in_=pairs[a, c][:].bitcast(word).rearrange("p u n -> p n u"),
             )
             return quads
 
@@ -177,39 +208,38 @@ def tile_moe_prv_lin_silu_kernel(
                 slots = slice(e * C - s0, (e + 1) * C - s0)
                 xq[a, e] = (codes[:, slots], scales[:, slots])
 
-        g1 = {}
-        for f in range(2):
-            for u in range(2):
-                g1[f, u] = cast_wu(1, f, u, nc.scalar.copy)
-        for u in range(2):
-            gather(0, u, 0)
-        for c, done in ((1, ((0, 0), (0, 1))), (2, ((1, 0),)), (3, ((1, 1),))):
-            for f, u in done:
-                wq[1, f, u] = quantize(f"wq1{f}{u}", g1[f, u], 2 * P)
-            f, u = done[-1]
-            gather(0, 0, c, f"wu_g1{f}{u}")
-            gather(0, 1, c)
+        order = ((0, 0), (1, 0), (0, 1), (1, 1))
+        after = ("wq001_codes", "wq011_codes", "wq001_scales", "wq011_scales")
+        g1 = [cast_wu(1, f, u, nc.scalar.copy, tag) for (f, u), tag in zip(order, after)]
+        gather(0, 0, 0)
+        gather(0, 1, 0)
+        gather(0, 0, 1)
+        gather(0, 1, 1)
+        for i, (f, u) in enumerate(order):
+            wq[1, f, u] = quantize(f"wq1{f}{u}", g1[i], 2 * P)
+            if i == 1:
+                gather(0, 0, 2, after[i])
+                gather(0, 1, 2)
         for u in range(2):
             for c in range(3):
                 project(1, u, c)
         for u in range(2):
-            for c in range(3):
+            for c in range(2):
                 gather(1, u, c)
         late = ("uq02_codes", "uq12_codes", "wq101_codes", "wq111_codes")
-        quads = {}
-        for c in range(4):
-            quads[0, c] = weave(0, c, late[c])
         for c in range(3):
-            quads[1, c] = weave(1, c)
-        for a in range(2):
-            for c in range(len(SLOT_CHUNKS[a])):
-                quantize_slots(a, c, quads[a, c])
+            quantize_slots(0, c, weave(0, c, late[c]))
+        quantize_slots(1, 0, weave(1, 0))
+        gather(1, 0, 2, "pairs10")
+        gather(1, 1, 2)
+        quantize_slots(1, 1, weave(1, 1))
+        quantize_slots(1, 2, weave(1, 2, None, nc.vector.tensor_copy, I32))
 
         y = [sb(f"y{r}", [P, S], F32) for r in range(ROW_BLOCKS)]
         for r in range(ROW_BLOCKS):
             cols = slice(r * P, (r + 1) * P)
             for e in range(E):
-                bank = psum.tile([P, C], F32, name="ybank", tag="ybank", bufs=3)
+                bank = bank_tile([P, C], e)
                 for a in range(2):
                     nc.tensor.matmul_mx(
                         out=bank[:],
@@ -224,15 +254,41 @@ def tile_moe_prv_lin_silu_kernel(
                     out=y[r][:, e * C : (e + 1) * C], in_=bank[:], func=SILU, bias=b_sb[:, r, e : e + 1]
                 )
 
-        for r in range(ROW_BLOCKS):
-            pieces = ((0, T),) if r + 1 < ROW_BLOCKS else ((0, 384), (384, 256))
-            for t0, n in pieces:
-                parts = []
-                for i in range(2):
-                    part = sb(f"part{r}{i}{t0}", [P, n], F32)
-                    picked = y[r][:].indirect(pos_sb[i][:, t0 // 16 : (t0 + n) // 16])
-                    nc.vector.tensor_tensor(part[:], picked, gate_sb[:, i, t0 : t0 + n], MULT)
-                    parts.append(part)
-                total = sb(f"total{r}{t0}", [P, n], F32)
-                nc.vector.tensor_tensor(total[:], parts[0][:], parts[1][:], ADD)
-                nc.sync.dma_start(out=out[r * P : (r + 1) * P, t0 : t0 + n], in_=total[:])
+        for r in range(ROW_BLOCKS - 1):
+            scaled = []
+            for i in range(2):
+                picked = sb(f"picked{r}{i}", [P, T], F32)
+                nc.vector.tensor_copy(out=picked[:], in_=y[r][:].indirect(pos_sb[i][:]))
+                turned = sb(f"turned{r}{i}", [P, BLOCKS, P], F32)
+                for b0, nb in BLOCK_GROUPS:
+                    bank = bank_tile([P, nb, P], len(taken) % 4)
+                    for k in range(nb):
+                        nc.tensor.transpose(bank[:, k, :], picked[:, (b0 + k) * P : (b0 + k + 1) * P], ident[:])
+                    for k in range(nb):
+                        col = 8 * i + b0 + k
+                        nc.scalar.activation(
+                            out=turned[:, b0 + k, :], in_=bank[:, k, :], func=COPY, scale=gate_cols[:, col : col + 1]
+                        )
+                scaled.append(turned)
+            total = sb(f"total{r}", [P, T], F32)
+            for b0, nb in BLOCK_GROUPS:
+                bank = bank_tile([P, nb, P], len(taken) % 4)
+                for k in range(nb):
+                    for i in range(2):
+                        nc.tensor.matmul(
+                            bank[:, k, :], scaled[i][:, b0 + k, :], ident[:], start=(i == 0), stop=(i == 1), is_transpose=True
+                        )
+                nc.scalar.copy(out=total[:, b0 * P : (b0 + nb) * P], in_=bank[:].rearrange("p k t -> p (k t)"))
+            nc.scalar.dma_start(out=out[r * P : (r + 1) * P, :], in_=total[:])
+
+        r = ROW_BLOCKS - 1
+        for t0, n in ((0, 384), (384, 256)):
+            parts = []
+            for i in range(2):
+                part = sb(f"part{i}{t0}", [P, n], F32)
+                picked = y[r][:].indirect(pos_sb[i][:, t0 // 16 : (t0 + n) // 16])
+                nc.vector.tensor_tensor(part[:], picked, gate_sb[:, i, t0 : t0 + n], MULT)
+                parts.append(part)
+            total = sb(f"last{t0}", [P, n], F32)
+            nc.vector.tensor_tensor(total[:], parts[0][:], parts[1][:], ADD)
+            nc.sync.dma_start(out=out[r * P : (r + 1) * P, t0 : t0 + n], in_=total[:])

from contextlib import ExitStack

import concourse.mybir as mybir
from concourse.masks import make_identity

M, K, T, E, C, N = 1024, 1024, 640, 5, 256, 384
S = E * C

F32 = mybir.dt.float32
BF16 = mybir.dt.bfloat16
I32 = mybir.dt.int32
U32 = mybir.dt.uint32
U16 = mybir.dt.uint16
U8 = mybir.dt.uint8
FP8X4 = mybir.dt.float8_e4m3fn_x4
MULT = mybir.AluOpType.mult
ADD = mybir.AluOpType.add
SILU = mybir.ActivationFunctionType.Silu
COPY = mybir.ActivationFunctionType.Copy

P = 128
PASS = 512
WINDOW = 704
TOKEN_CHUNKS = ((0, 256), (256, 256), (512, 128))
SLOT_CHUNKS = (
    ((0, 512), (512, 256), (768, 512)),
    ((0, 512), (512, 512), (1024, 256)),
)
U_LOADS = (((0, T),), ((0, 384), (384, 256)))
U_CASTS = (((0, 0, 256, 0), (1, 128, 256, 1), (1, 0, 128, 0), (2, 0, 128, 1)), ((0, 0, 256, 0), (1, 0, 128, 1), (1, 128, 256, 0), (2, 0, 128, 1)))
V_EVAC = ((0, 1),)
ROW_BLOCKS = N // P
BLOCKS = T // P
BLOCK_GROUPS = ((0, 3), (3, 2))

FLOPS = 2 * M * K * T + 2 * K * N * S
BYTES = 4 * (M * T + M * K + N * E + 2 * T + N * T) + E * K * N + E * K * N // 32 + 2 * P * (S + 2 * T) // 16


def tile_moe_prv_lin_silu_kernel(
    tc, uT, wu, w_words, w_scales, b, gate, offs, pos1, pos2, out
):
    nc = tc.nc
    with ExitStack() as ctx:
        keep = ctx.enter_context(tc.tile_pool(name="keep", bufs=1))
        psum = ctx.enter_context(tc.psum_pool(name="psum", bufs=1))

        def sb(name, shape, dtype, tag=None):
            return keep.tile(shape, dtype, name=name, tag=tag or name, align_bytes=64)

        def quantize(name, grouped, width):
            codes = sb(name + "_codes", [P, width], U32)
            scales = sb(name + "_scales", [P, width], U8)
            nc.vector.quantize_mx(out=codes[:].bitcast(FP8X4), scales=scales[:], in_=grouped)
            return codes, scales

        taken = []

        def bank_tile(shape, bank=None):
            bank = len(taken) % 8 if bank is None else bank
            taken.append(bank)
            return psum.tile(shape, F32, name=f"bank{bank}", tag=f"bank{bank}")

        wu_raw = {}
        u_raw = {}

        def load_wu(a, f):
            raw = sb(f"wu_raw{a}{f}", [P, 4, PASS], F32)
            rows = wu[f * PASS : (f + 1) * PASS, a * PASS : (a + 1) * PASS]
            nc.sync.dma_start(out=raw[:], in_=rows.rearrange("(p j) c -> p j c", j=4))
            wu_raw[a, f] = raw

        load_wu(0, 0)
        load_wu(0, 1)
        for f in range(2):
            for t0, n in U_LOADS[f]:
                raw = sb(f"u_raw{f}{t0}", [P, 4, n], F32)
                rows = uT[f * PASS : (f + 1) * PASS, t0 : t0 + n]
                nc.sync.dma_start(out=raw[:], in_=rows.rearrange("(p j) t -> p j t", j=4))
                for t in range(t0, t0 + n, P):
                    u_raw[f, t] = (raw, t0)
        offs_sb = sb("offs_sb", [P, S // 16], U16)
        nc.sync.dma_start(offs_sb[:], offs)
        gate_rows = sb("gate_rows", [P, P], F32)
        nc.gpsimd.memset(gate_rows[:], 0.0)
        for i in range(2):
            nc.sync.dma_start(
                out=gate_rows[8 * i : 8 * i + BLOCKS, :], in_=gate[i, 0, :].rearrange("(c p) -> c p", p=P)
            )
        ident = sb("ident", [P, P], F32)
        make_identity(nc, ident[:])
        load_wu(1, 0)
        load_wu(1, 1)

        w_sb = []
        for e in range(E):
            words = sb(f"w_words{e}", [P, 2, N], U32)
            nc.sync.dma_start(
                out=words[:].bitcast(I32),
                in_=w_words[e].rearrange("a p n r -> p a (n r)").bitcast(I32),
            )
            w_sb.append(words)
        w_sc = sb("w_sc", [P, 2 * E, N], U8)
        nc.gpsimd.memset(w_sc[:].bitcast(I32), 0)
        sc_rows = w_scales.rearrange("e a (g r) n -> r g (e a) n", r=4)
        for r in range(4):
            nc.sync.dma_start(out=w_sc[r:P:32].bitcast(I32), in_=sc_rows[r].bitcast(I32))
        b_sb = sb("b_sb", [P, ROW_BLOCKS, E], F32)
        nc.sync.dma_start(out=b_sb[:], in_=b.rearrange("(r p) e -> p r e", p=P))
        pos_sb = []
        for i, pos in enumerate((pos1, pos2)):
            lst = sb(f"pos_sb{i}", [P, T // 16], U16)
            nc.sync.dma_start(lst[:], pos)
            pos_sb.append(lst)
        gate_sb = sb("gate_sb", [P, 2, T], F32)
        nc.sync.dma_start(out=gate_sb[:], in_=gate[:, 0:P, :].rearrange("i p t -> p i t"))

        win = {}
        for a in range(2):
            for u in range(2):
                tile = sb(f"win{a}{u}", [P, 2 * WINDOW], BF16)
                nc.gpsimd.memset(tile[:, 2 * T :], 0.0)
                win[a, u] = tile

        wq = {}
        uq = {}

        def cast_wu(a, f, u, copy, tag=None):
            grouped = sb(f"wu_g{a}{f}{u}", [P, 2, P, 4], BF16, tag)
            src = wu_raw[a, f][:].rearrange("p j (m t) -> p m j t", t=4)[:, :, :, 2 * u : 2 * u + 2]
            copy(out=grouped[:].rearrange("p t m j -> p m j t"), in_=src)
            return grouped[:].rearrange("p t m j -> p (t m j)")

        def cast_u(f):
            grouped = [sb(f"u_g{f}{c}", [P, n, 4], BF16) for c, (t0, n) in enumerate(TOKEN_CHUNKS)]
            for c, lo, hi, engine in U_CASTS[f]:
                raw, first = u_raw[f, TOKEN_CHUNKS[c][0] + lo]
                t0 = TOKEN_CHUNKS[c][0] - first
                (nc.vector.tensor_copy, nc.scalar.copy)[engine](
                    out=grouped[c][:, lo:hi, :].rearrange("p (c i) j -> p c j i", i=4),
                    in_=raw[:, :, t0 + lo : t0 + hi].rearrange("p j (c i) -> p c j i", i=4),
                )
            return [g[:].rearrange("p t j -> p (t j)") for g in grouped]

        def project(a, u, c, copy=nc.scalar.copy):
            t0, n = TOKEN_CHUNKS[c]
            bank = bank_tile([P, 2, n])
            for tt in range(2):
                cols = slice(tt * P, (tt + 1) * P)
                for f in range(2):
                    nc.tensor.matmul_mx(
                        out=bank[:, tt, :],
                        lhsT=wq[a, f, u][0][:, cols].bitcast(FP8X4),
                        lhsT_scale=wq[a, f, u][1][:, cols],
                        rhs=uq[f, c][0][:].bitcast(FP8X4),
                        rhs_scale=uq[f, c][1][:],
                        start=(f == 0),
                        stop=(f == 1),
                    )
            copy(
                out=win[a, u][:, 2 * t0 : 2 * (t0 + n)].rearrange("p (n t) -> p n t", t=2),
                in_=bank[:].rearrange("p t n -> p n t"),
            )

        both = (nc.vector.tensor_copy, nc.scalar.copy)
        for f in range(2):
            g = [cast_wu(0, f, u, both[u]) for u in range(2)]
            for u in range(2):
                wq[0, f, u] = quantize(f"wq0{f}{u}", g[u], 2 * P)
        for f in range(2):
            g = cast_u(f)
            for c in range(3):
                uq[f, c] = quantize(f"uq{f}{c}", g[c], TOKEN_CHUNKS[c][1])
        for u in range(2):
            for c in range(3):
                project(0, u, c, nc.vector.tensor_copy if (u, c) in V_EVAC else nc.scalar.copy)

        gate_bank = bank_tile([P, P], 5)
        nc.tensor.transpose(gate_bank[:], gate_rows[:], ident[:])
        gate_cols = sb("gate_cols", [P, 16], F32)
        nc.scalar.copy(out=gate_cols[:], in_=gate_bank[:, 0:16])

        pairs = {}
        xq = {}

        def gather(a, u, c, tag=None):
            s0, n = SLOT_CHUNKS[a][c]
            if u == 0:
                pairs[a, c] = sb(f"pairs{a}{c}", [P, 2, n], U32, tag)
            nc.vector.tensor_copy(
                out=pairs[a, c][:, u, :],
                in_=win[a, u][:].bitcast(U32).indirect(offs_sb[:, s0 // 16 : (s0 + n) // 16]),
            )

        def weave(a, c, tag=None, copy=nc.scalar.copy, word=U32):
            n = SLOT_CHUNKS[a][c][1]
            quads = sb(f"quads{a}{c}", [P, 4 * n], BF16, tag)
            copy(
                out=quads[:].bitcast(word).rearrange("p (n u) -> p n u", u=2),
                in_=pairs[a, c][:].bitcast(word).rearrange("p u n -> p n u"),
            )
            return quads

        def quantize_slots(a, c, quads):
            s0, n = SLOT_CHUNKS[a][c]
            codes, scales = quantize(f"xq{a}{c}", quads[:], n)
            for e in range(s0 // C, (s0 + n) // C):
                slots = slice(e * C - s0, (e + 1) * C - s0)
                xq[a, e] = (codes[:, slots], scales[:, slots])

        order = ((0, 0), (1, 0), (0, 1), (1, 1))
        after = ("wq001_codes", "wq011_codes", "wq001_scales", "wq011_scales")
        g1 = [cast_wu(1, f, u, nc.scalar.copy, tag) for (f, u), tag in zip(order, after)]
        gather(0, 0, 0)
        gather(0, 1, 0)
        gather(0, 0, 1)
        gather(0, 1, 1)
        for i, (f, u) in enumerate(order):
            wq[1, f, u] = quantize(f"wq1{f}{u}", g1[i], 2 * P)
            if i == 1:
                gather(0, 0, 2, after[i])
                gather(0, 1, 2)
        for u in range(2):
            for c in range(3):
                project(1, u, c)
        for u in range(2):
            for c in range(2):
                gather(1, u, c)
        late = ("uq02_codes", "uq12_codes", "wq101_codes", "wq111_codes")
        for c in range(3):
            quantize_slots(0, c, weave(0, c, late[c]))
        quantize_slots(1, 0, weave(1, 0))
        gather(1, 0, 2, "pairs10")
        gather(1, 1, 2)
        quantize_slots(1, 1, weave(1, 1))
        quantize_slots(1, 2, weave(1, 2, None, nc.vector.tensor_copy, I32))

        y = [sb(f"y{r}", [P, S], F32) for r in range(ROW_BLOCKS)]
        for r in range(ROW_BLOCKS):
            cols = slice(r * P, (r + 1) * P)
            for e in range(E):
                bank = bank_tile([P, C], e)
                for a in range(2):
                    nc.tensor.matmul_mx(
                        out=bank[:],
                        lhsT=w_sb[e][:, a, cols].bitcast(FP8X4),
                        lhsT_scale=w_sc[:, 2 * e + a, cols],
                        rhs=xq[a, e][0].bitcast(FP8X4),
                        rhs_scale=xq[a, e][1],
                        start=(a == 0),
                        stop=(a == 1),
                    )
                nc.scalar.activation(
                    out=y[r][:, e * C : (e + 1) * C], in_=bank[:], func=SILU, bias=b_sb[:, r, e : e + 1]
                )

        for r in range(ROW_BLOCKS - 1):
            scaled = []
            for i in range(2):
                picked = sb(f"picked{r}{i}", [P, T], F32)
                nc.vector.tensor_copy(out=picked[:], in_=y[r][:].indirect(pos_sb[i][:]))
                turned = sb(f"turned{r}{i}", [P, BLOCKS, P], F32)
                for b0, nb in BLOCK_GROUPS:
                    bank = bank_tile([P, nb, P], len(taken) % 4)
                    for k in range(nb):
                        nc.tensor.transpose(bank[:, k, :], picked[:, (b0 + k) * P : (b0 + k + 1) * P], ident[:])
                    for k in range(nb):
                        col = 8 * i + b0 + k
                        nc.scalar.activation(
                            out=turned[:, b0 + k, :], in_=bank[:, k, :], func=COPY, scale=gate_cols[:, col : col + 1]
                        )
                scaled.append(turned)
            total = sb(f"total{r}", [P, T], F32)
            for b0, nb in BLOCK_GROUPS:
                bank = bank_tile([P, nb, P], len(taken) % 4)
                for k in range(nb):
                    for i in range(2):
                        nc.tensor.matmul(
                            bank[:, k, :], scaled[i][:, b0 + k, :], ident[:], start=(i == 0), stop=(i == 1), is_transpose=True
                        )
                nc.scalar.copy(out=total[:, b0 * P : (b0 + nb) * P], in_=bank[:].rearrange("p k t -> p (k t)"))
            nc.scalar.dma_start(out=out[r * P : (r + 1) * P, :], in_=total[:])

        r = ROW_BLOCKS - 1
        for t0, n in ((0, 384), (384, 256)):
            parts = []
            for i in range(2):
                part = sb(f"part{i}{t0}", [P, n], F32)
                picked = y[r][:].indirect(pos_sb[i][:, t0 // 16 : (t0 + n) // 16])
                nc.vector.tensor_tensor(part[:], picked, gate_sb[:, i, t0 : t0 + n], MULT)
                parts.append(part)
            total = sb(f"last{t0}", [P, n], F32)
            nc.vector.tensor_tensor(total[:], parts[0][:], parts[1][:], ADD)
            nc.sync.dma_start(out=out[r * P : (r + 1) * P, t0 : t0 + n], in_=total[:])
